import numpy as np
import ml_dtypes


def mxq(x, axis, fmt="e4m3"):
    dtype, down = {"e4m3": (ml_dtypes.float8_e4m3fn, 7), "e5m2": (ml_dtypes.float8_e5m2, 14)}[fmt]
    v = np.moveaxis(np.asarray(x, np.float32).astype(ml_dtypes.bfloat16).astype(np.float64), axis, -1)
    blocks = v.reshape(v.shape[:-1] + (-1, 32))
    amax = np.abs(blocks).max(-1, keepdims=True)
    byte = np.maximum(np.where(amax > 0, np.frexp(amax)[1] - 1 + 127, 0) - down, 1)
    scale = np.exp2(byte - 127.0)
    codes = (blocks / scale).astype(np.float32).astype(dtype).astype(np.float64)
    return np.moveaxis((codes * scale).reshape(v.shape), -1, axis)


WIDE = False


def mx_kscale(k):
    if not WIDE:
        return np.ones(k)
    levels = np.array([10, -10, 5, -5, 0])
    if k % 512:
        return np.exp2(np.random.permutation(np.resize(levels, k // 32))).repeat(32)
    a = np.empty((k // 512, 16))
    for p in range(k // 512):
        a[p, :8] = np.random.permutation(np.resize(levels, 8))
        for g in range(8):
            far = levels[np.abs(levels - a[p, g]) >= 10]
            a[p, g + 8] = far[np.random.randint(len(far))]
    return np.exp2(a.ravel()).repeat(32)


def f64(x):
    return np.asarray(x).astype(np.float64)


def striped(idx):
    return np.tile(idx.reshape(-1, 16).T, (8, 1)).astype(np.uint16)


def unstriped(offs):
    return offs[:16].T.reshape(-1).astype(np.int64)


def pack_weight(w):
    k, n = w.shape
    w = f64(np.asarray(w, np.float32).astype(ml_dtypes.bfloat16)).reshape(k // 32, 32, n)
    amax = np.abs(w).max(1)
    byte = np.clip(np.where(amax > 0, np.frexp(amax)[1] - 1 + 127 - 7, 1), 1, 254)
    scaled = (w * np.exp2(127.0 - byte)[:, None, :]).reshape(k, n).astype(np.float32)
    words = np.ascontiguousarray(scaled.reshape(k // 512, 128, 4, n).transpose(0, 1, 3, 2)).astype(ml_dtypes.float8_e4m3fn).view(np.uint8)
    return words, np.ascontiguousarray(byte.astype(np.uint8).reshape(k // 512, 16, n))


def unpack_weight(words, scales):
    g, p, n, _ = words.shape
    vals = np.ascontiguousarray(words).view(ml_dtypes.float8_e4m3fn).astype(np.float64) * np.repeat(np.exp2(scales.astype(np.float64) - 127.0), 8, axis=1)[..., None]
    return vals.transpose(0, 1, 3, 2).reshape(g * 512, n)


def silu(v):
    return v / (1.0 + np.exp(-np.maximum(v, -700.0)))


K, T, S, V, N = 512, 1024, 512, 256, 256


def setup_inputs():
    n = np.random.standard_normal
    s = mx_kscale(K)[:, None]
    packed_xT = pack_weight(n((K, T)) * s)
    return {
        "x_words": packed_xT[0],
        "x_scales": packed_xT[1],
        "w1": (n((K, N)) / np.sqrt(K) / s).astype(np.float32),
        "w2": (n((K, N)) / np.sqrt(K) / s).astype(np.float32),
        "w3": (n((K, N)) / np.sqrt(K) / s).astype(np.float32),
        "offs": striped(np.random.permutation(T)[:S]),
        "cen": striped(np.random.permutation(S)[:V]),
        "pos1": striped(np.random.permutation(S)[:V]),
        "pos2": striped(np.random.permutation(S)[:V]),
        "pos3": striped(np.random.permutation(S)[:V]),
    }


def reference(x_words, x_scales, w1, w2, w3, offs, cen, pos1, pos2, pos3):
    xq = unpack_weight(x_words, x_scales)[:, unstriped(offs)]
    h = mxq(f64(w3), 0, "e4m3").T @ xq
    g = mxq(f64(w1), 0, "e4m3").T @ xq
    gc = g[:, unstriped(cen)]
    s = mxq(f64(w2), 0, "e4m3").T @ xq
    sc = s[:, unstriped(cen)]
    return silu(h[:, unstriped(pos1)] * gc + sc) + silu(h[:, unstriped(pos2)] * gc + sc) + silu(h[:, unstriped(pos3)] * gc + sc)

@@ -1,0 +1,159 @@
+from contextlib import ExitStack
+
+import concourse.mybir as mybir
+from concourse.masks import make_identity
+
+K, T, S, V, N = 512, 1024, 512, 256, 256
+P = 128
+PACK = 4
+D = 3
+TILES = N // P
+FLOPS = 3 * 2 * K * N * S
+
+F32 = mybir.dt.float32
+BF16 = mybir.dt.bfloat16
+I32 = mybir.dt.int32
+U32 = mybir.dt.uint32
+U16 = mybir.dt.uint16
+U8 = mybir.dt.uint8
+FP8X4 = mybir.dt.float8_e4m3fn_x4
+MULT = mybir.AluOpType.mult
+ADD = mybir.AluOpType.add
+SILU = mybir.ActivationFunctionType.Silu
+
+
+def tile_picked_filmg_silu_p_kernel(
+    tc, x_words, x_scales, w1, w2, w3, offs, cen, pos1, pos2, pos3, out
+):
+    nc = tc.nc
+    with ExitStack() as ctx:
+        keep = ctx.enter_context(tc.tile_pool(name="keep", bufs=1))
+        prod = ctx.enter_context(tc.psum_pool(name="prod", bufs=3))
+        pre = ctx.enter_context(tc.psum_pool(name="pre", bufs=3))
+        total = ctx.enter_context(tc.psum_pool(name="total", bufs=1))
+
+        def load_list(src, name):
+            t = keep.tile(list(src.shape), U16, name=name)
+            nc.sync.dma_start(t[:], src)
+            return t
+
+        offs_t = load_list(offs, "offs_t")
+        xw = keep.tile([P, T], I32, name="xw", align_bytes=64)
+        nc.sync.dma_start(xw[:], x_words[0].rearrange("p n t -> p (n t)").bitcast(I32))
+
+        xs = keep.tile([P, T], U8, name="xs", align_bytes=64)
+        nc.vector.memset(xs[:].bitcast(I32), 0)
+        for q in range(4):
+            nc.scalar.dma_start(
+                xs[32 * q : 32 * q + 4, :].bitcast(I32), x_scales[0, 4 * q : 4 * q + 4, :].bitcast(I32)
+            )
+
+        warm = keep.tile([P, 8], F32, name="warm")
+        nc.gpsimd.memset(warm[:, 0:1], 0.0)
+        nc.scalar.activation(warm[:, 4:5], warm[:, 0:1], SILU)
+
+        def load_w(w, name):
+            t = keep.tile([P, PACK, N], F32, name=name)
+            nc.sync.dma_start(t[:], w.rearrange("(p j) n -> p j n", j=PACK))
+            return t
+
+        w1_raw = load_w(w1, "w1_raw")
+        w3_raw = load_w(w3, "w3_raw")
+        cen_t = load_list(cen, "cen_t")
+        pos_t = [load_list(pos1, "pos1_t")]
+        w2_raw = load_w(w2, "w2_raw")
+        pos_t.append(load_list(pos2, "pos2_t"))
+        pos_t.append(load_list(pos3, "pos3_t"))
+
+        ident = keep.tile([P, P], F32, name="ident")
+        make_identity(nc, ident[:])
+
+        xq_s = keep.tile([P, S], U8, name="xq_s", align_bytes=64)
+        nc.vector.tensor_copy(xq_s[:], xs[:].indirect(offs_t[:]))
+        xq_w = keep.tile([P, S], U32, name="xq_w", align_bytes=64)
+        nc.vector.tensor_copy(xq_w[:], xw[:].bitcast(U32).indirect(offs_t[:]))
+
+        def cast(raw, m, name, on_vector):
+            t = keep.tile([P, P, PACK], BF16, name=name, align_bytes=64)
+            dst = t[:].rearrange("p (c i) j -> p c j i", i=4)
+            src = raw[:, :, m * P : (m + 1) * P].rearrange("p j (c i) -> p c j i", i=4)
+            if on_vector:
+                nc.vector.tensor_copy(dst, src)
+            else:
+                nc.scalar.copy(dst, src)
+            return t
+
+        def product(grouped, name):
+            codes = keep.tile([P, P], U32, name=name + "_codes", align_bytes=64)
+            scales = keep.tile([P, P], U8, name=name + "_scales", align_bytes=64)
+            nc.vector.quantize_mx(
+                out=codes[:].bitcast(FP8X4), scales=scales[:], in_=grouped[:].rearrange("p c j -> p (c j)")
+            )
+            acc = prod.tile([P, S], F32, name="acc")
+            nc.tensor.matmul_mx(
+                out=acc[:], lhsT=codes[:].bitcast(FP8X4), lhsT_scale=scales[:],
+                rhs=xq_w[:].bitcast(FP8X4), rhs_scale=xq_s[:], start=True, stop=True,
+            )
+            res = keep.tile([P, S], F32, name=name)
+            nc.scalar.copy(res[:], acc[:])
+            return res
+
+        c10 = cast(w1_raw, 0, "c10", True)
+        c11 = cast(w1_raw, 1, "c11", False)
+        g = [product(c10, "g0"), product(c11, "g1")]
+        c30 = cast(w3_raw, 0, "c30", True)
+        h = [product(c30, "h0")]
+        c31 = cast(w3_raw, 1, "c31", False)
+
+        def fetch(res, name):
+            t = keep.tile([P, V], F32, name=name)
+            nc.vector.tensor_copy(t[:], res[:].indirect(cen_t[:]))
+            return t
+
+        gc = [fetch(g[0], "gc0"), fetch(g[1], "gc1")]
+        c20 = cast(w2_raw, 0, "c20", False)
+        h.append(product(c31, "h1"))
+        s = [product(c20, "s0")]
+        c21 = cast(w2_raw, 1, "c21", False)
+
+        def scaled(m, d):
+            t = keep.tile([P, V], F32, name="t%d%d" % (m, d))
+            nc.vector.tensor_tensor(t[:], h[m][:].indirect(pos_t[d][:]), gc[m][:], MULT)
+            return t
+
+        def through_tensor(m, d, t, sc, sums, first, last):
+            u = pre.tile([P, 2, P], F32, name="u")
+            for c in range(2):
+                nc.tensor.matmul(u[:, c, :], sc[:, c * P : (c + 1) * P], ident[:], start=True, stop=False, is_transpose=True)
+                nc.tensor.matmul(u[:, c, :], t[:, c * P : (c + 1) * P], ident[:], start=False, stop=True, is_transpose=True)
+            a = keep.tile([P, 2, P], F32, name="a%d%d" % (m, d))
+            nc.scalar.activation(a[:], u[:], SILU)
+            for c in range(2):
+                nc.tensor.matmul(sums[c][:], a[:, c, :], ident[:], start=first, stop=last, is_transpose=True)
+
+        t0 = [scaled(0, 0)]
+        s.append(product(c21, "s1"))
+        t0.append(scaled(0, 1))
+        sc0 = fetch(s[0], "sc0")
+        t0.append(scaled(0, 2))
+        sums = [total.tile([P, P], F32, name="sum%d" % c) for c in range(2)]
+        for d in range(D):
+            through_tensor(0, d, t0[d], sc0, sums, d == 0, d == D - 1)
+        o0 = keep.tile([P, V], F32, name="o0")
+        for c in range(2):
+            nc.scalar.copy(o0[:, c * P : (c + 1) * P], sums[c][:])
+        nc.sync.dma_start(out[0:P, :], o0[:])
+
+        sc1 = fetch(s[1], "sc1")
+        t1 = [scaled(1, d) for d in range(D)]
+        sums = [total.tile([P, P], F32, name="sum%d" % c) for c in range(2)]
+        for d in range(D - 1):
+            through_tensor(1, d, t1[d], sc1, sums, d == 0, d == D - 2)
+        u = keep.tile([P, V], F32, name="u_last")
+        nc.vector.tensor_tensor(u[:], t1[D - 1][:], sc1[:], ADD)
+        a = keep.tile([P, V], F32, name="a_last")
+        nc.scalar.activation(a[:], u[:], SILU)
+        o1 = keep.tile([P, V], F32, name="o1")
+        for c in range(2):
+            nc.vector.tensor_tensor(o1[:, c * P : (c + 1) * P], sums[c][:], a[:, c * P : (c + 1) * P], ADD)
+        nc.sync.dma_start(out[P : 2 * P, :], o1[:])

@@ -7,7 +7,7 @@ K, T, S, V, N = 512, 1024, 512, 256, 256
 P = 128
 PACK = 4
 D = 3
-TILES = N // P
+HALF = S // 2
 FLOPS = 3 * 2 * K * N * S
 
 F32 = mybir.dt.float32
@@ -28,9 +28,8 @@ def tile_picked_filmg_silu_p_kernel(
     nc = tc.nc
     with ExitStack() as ctx:
         keep = ctx.enter_context(tc.tile_pool(name="keep", bufs=1))
-        prod = ctx.enter_context(tc.psum_pool(name="prod", bufs=3))
-        pre = ctx.enter_context(tc.psum_pool(name="pre", bufs=3))
-        total = ctx.enter_context(tc.psum_pool(name="total", bufs=1))
+        banks = ctx.enter_context(tc.psum_pool(name="banks", bufs=6))
+        total = ctx.enter_context(tc.psum_pool(name="total", bufs=2))
 
         def load_list(src, name):
             t = keep.tile(list(src.shape), U16, name=name)
@@ -38,122 +37,139 @@ def tile_picked_filmg_silu_p_kernel(
             return t
 
         offs_t = load_list(offs, "offs_t")
-        xw = keep.tile([P, T], I32, name="xw", align_bytes=64)
-        nc.sync.dma_start(xw[:], x_words[0].rearrange("p n t -> p (n t)").bitcast(I32))
 
+        xw = keep.tile([P, T], I32, name="xw", align_bytes=64)
+        nc.scalar.dma_start(xw[:], x_words[0].rearrange("p n t -> p (n t)").bitcast(I32))
         xs = keep.tile([P, T], U8, name="xs", align_bytes=64)
         nc.vector.memset(xs[:].bitcast(I32), 0)
         for q in range(4):
-            nc.scalar.dma_start(
+            nc.sync.dma_start(
                 xs[32 * q : 32 * q + 4, :].bitcast(I32), x_scales[0, 4 * q : 4 * q + 4, :].bitcast(I32)
             )
 
-        warm = keep.tile([P, 8], F32, name="warm")
-        nc.gpsimd.memset(warm[:, 0:1], 0.0)
-        nc.scalar.activation(warm[:, 4:5], warm[:, 0:1], SILU)
-
-        def load_w(w, name):
-            t = keep.tile([P, PACK, N], F32, name=name)
-            nc.sync.dma_start(t[:], w.rearrange("(p j) n -> p j n", j=PACK))
+        def load_w(w, lo, hi, name):
+            t = keep.tile([P, PACK, hi - lo], F32, name=name)
+            nc.sync.dma_start(t[:], w[:, lo:hi].rearrange("(p j) n -> p j n", j=PACK))
             return t
 
-        w1_raw = load_w(w1, "w1_raw")
-        w3_raw = load_w(w3, "w3_raw")
+        w1_raw = [load_w(w1, 0, P, "w1_raw0"), load_w(w1, P, N, "w1_raw1")]
+        w3_raw = load_w(w3, 0, N, "w3_raw")
+        w2_raw = load_w(w2, 0, N, "w2_raw")
         cen_t = load_list(cen, "cen_t")
-        pos_t = [load_list(pos1, "pos1_t")]
-        w2_raw = load_w(w2, "w2_raw")
-        pos_t.append(load_list(pos2, "pos2_t"))
-        pos_t.append(load_list(pos3, "pos3_t"))
+        pos_t = [load_list(pos1, "pos1_t"), load_list(pos2, "pos2_t"), load_list(pos3, "pos3_t")]
+
+        warm = keep.tile([P, 8], F32, name="warm")
+        nc.vector.memset(warm[:, 0:1], 0.0)
+        nc.scalar.activation(warm[:, 4:5], warm[:, 0:1], SILU)
 
         ident = keep.tile([P, P], F32, name="ident")
         make_identity(nc, ident[:])
 
-        xq_s = keep.tile([P, S], U8, name="xq_s", align_bytes=64)
-        nc.vector.tensor_copy(xq_s[:], xs[:].indirect(offs_t[:]))
-        xq_w = keep.tile([P, S], U32, name="xq_w", align_bytes=64)
-        nc.vector.tensor_copy(xq_w[:], xw[:].bitcast(U32).indirect(offs_t[:]))
-
-        def cast(raw, m, name, on_vector):
-            t = keep.tile([P, P, PACK], BF16, name=name, align_bytes=64)
+        def cast(raw, name, on_vector, tag=None):
+            t = keep.tile([P, raw.shape[2], PACK], BF16, name=name, tag=tag or name, align_bytes=64)
             dst = t[:].rearrange("p (c i) j -> p c j i", i=4)
-            src = raw[:, :, m * P : (m + 1) * P].rearrange("p j (c i) -> p c j i", i=4)
+            src = raw.rearrange("p j (c i) -> p c j i", i=4)
             if on_vector:
                 nc.vector.tensor_copy(dst, src)
             else:
                 nc.scalar.copy(dst, src)
             return t
 
-        def product(grouped, name):
-            codes = keep.tile([P, P], U32, name=name + "_codes", align_bytes=64)
-            scales = keep.tile([P, P], U8, name=name + "_scales", align_bytes=64)
+        def quantize(grouped, name):
+            codes = keep.tile([P, grouped.shape[1]], U32, name=name + "_codes", tag=name + "_codes", align_bytes=64)
+            scales = keep.tile([P, grouped.shape[1]], U8, name=name + "_scales", align_bytes=64)
             nc.vector.quantize_mx(
                 out=codes[:].bitcast(FP8X4), scales=scales[:], in_=grouped[:].rearrange("p c j -> p (c j)")
             )
-            acc = prod.tile([P, S], F32, name="acc")
+            return codes[:], scales[:]
+
+        def pick(window, dtype, half, name, tag=None):
+            t = keep.tile([P, HALF], dtype, name=name, tag=tag or name, align_bytes=64)
+            cols = HALF // 16
+            nc.vector.tensor_copy(t[:], window.indirect(offs_t[:, half * cols : (half + 1) * cols]))
+            return t
+
+        xq_w = [pick(xw[:].bitcast(U32), U32, 0, "xq_w0")]
+        xq_s = [pick(xs[:], U8, 0, "xq_s0"), pick(xs[:], U8, 1, "xq_s1")]
+        q10 = quantize(cast(w1_raw[0][:], "c10", False, "shared"), "g0")
+        xq_w.append(pick(xw[:].bitcast(U32), U32, 1, "xq_w1", "shared"))
+
+        def multiply(acc, q, half):
             nc.tensor.matmul_mx(
-                out=acc[:], lhsT=codes[:].bitcast(FP8X4), lhsT_scale=scales[:],
-                rhs=xq_w[:].bitcast(FP8X4), rhs_scale=xq_s[:], start=True, stop=True,
+                out=acc, lhsT=q[0].bitcast(FP8X4), lhsT_scale=q[1],
+                rhs=xq_w[half][:].bitcast(FP8X4), rhs_scale=xq_s[half][:], start=True, stop=True,
             )
-            res = keep.tile([P, S], F32, name=name)
+
+        def product(q, name):
+            acc = banks.tile([P, S], F32, name="bank")
+            for half in range(2):
+                multiply(acc[:, half * HALF : (half + 1) * HALF], q, half)
+            res = keep.tile([P, S], F32, name=name, tag=name, align_bytes=64)
             nc.scalar.copy(res[:], acc[:])
             return res
 
-        c10 = cast(w1_raw, 0, "c10", True)
-        c11 = cast(w1_raw, 1, "c11", False)
-        g = [product(c10, "g0"), product(c11, "g1")]
-        c30 = cast(w3_raw, 0, "c30", True)
-        h = [product(c30, "h0")]
-        c31 = cast(w3_raw, 1, "c31", False)
+        c11 = cast(w1_raw[1][:], "c11", False)
+        g0 = keep.tile([P, S], F32, name="g0")
+        for half in range(2):
+            acc = banks.tile([P, S], F32, name="bank")
+            multiply(acc[:, 0:HALF], q10, half)
+            nc.scalar.copy(g0[:, half * HALF : (half + 1) * HALF], acc[:, 0:HALF])
+        q11 = quantize(c11, "g1")
+        q3 = quantize(cast(w3_raw[:], "c3", True), "h")
+        g = [g0, product(q11, "g1")]
+        c20 = cast(w2_raw[:, :, 0:P], "c20", False, "g1_codes")
+        h = [product([x[:, 0:P] for x in q3], "h0")]
+        h.append(product([x[:, P:N] for x in q3], "h1"))
+        c21 = cast(w2_raw[:, :, P:N], "c21", False, "h_codes")
 
         def fetch(res, name):
             t = keep.tile([P, V], F32, name=name)
             nc.vector.tensor_copy(t[:], res[:].indirect(cen_t[:]))
             return t
 
-        gc = [fetch(g[0], "gc0"), fetch(g[1], "gc1")]
-        c20 = cast(w2_raw, 0, "c20", False)
-        h.append(product(c31, "h1"))
-        s = [product(c20, "s0")]
-        c21 = cast(w2_raw, 1, "c21", False)
-
-        def scaled(m, d):
-            t = keep.tile([P, V], F32, name="t%d%d" % (m, d))
+        def scaled(m, d, tag=None):
+            t = keep.tile([P, V], F32, name="t%d%d" % (m, d), tag=tag or "t%d%d" % (m, d), align_bytes=64)
             nc.vector.tensor_tensor(t[:], h[m][:].indirect(pos_t[d][:]), gc[m][:], MULT)
             return t
 
-        def through_tensor(m, d, t, sc, sums, first, last):
-            u = pre.tile([P, 2, P], F32, name="u")
+        def turn(dst, src, start, stop):
             for c in range(2):
-                nc.tensor.matmul(u[:, c, :], sc[:, c * P : (c + 1) * P], ident[:], start=True, stop=False, is_transpose=True)
-                nc.tensor.matmul(u[:, c, :], t[:, c * P : (c + 1) * P], ident[:], start=False, stop=True, is_transpose=True)
-            a = keep.tile([P, 2, P], F32, name="a%d%d" % (m, d))
-            nc.scalar.activation(a[:], u[:], SILU)
-            for c in range(2):
-                nc.tensor.matmul(sums[c][:], a[:, c, :], ident[:], start=first, stop=last, is_transpose=True)
+                nc.tensor.matmul(
+                    dst[:, c * P : (c + 1) * P], src[:, c * P : (c + 1) * P], ident[:],
+                    start=start and c == 0, stop=stop and c == 1, is_transpose=True,
+                )
 
-        t0 = [scaled(0, 0)]
-        s.append(product(c21, "s1"))
-        t0.append(scaled(0, 1))
-        sc0 = fetch(s[0], "sc0")
-        t0.append(scaled(0, 2))
-        sums = [total.tile([P, P], F32, name="sum%d" % c) for c in range(2)]
-        for d in range(D):
-            through_tensor(0, d, t0[d], sc0, sums, d == 0, d == D - 1)
-        o0 = keep.tile([P, V], F32, name="o0")
-        for c in range(2):
-            nc.scalar.copy(o0[:, c * P : (c + 1) * P], sums[c][:])
-        nc.sync.dma_start(out[0:P, :], o0[:])
-
-        sc1 = fetch(s[1], "sc1")
-        t1 = [scaled(1, d) for d in range(D)]
-        sums = [total.tile([P, P], F32, name="sum%d" % c) for c in range(2)]
-        for d in range(D - 1):
-            through_tensor(1, d, t1[d], sc1, sums, d == 0, d == D - 2)
-        u = keep.tile([P, V], F32, name="u_last")
-        nc.vector.tensor_tensor(u[:], t1[D - 1][:], sc1[:], ADD)
-        a = keep.tile([P, V], F32, name="a_last")
-        nc.scalar.activation(a[:], u[:], SILU)
-        o1 = keep.tile([P, V], F32, name="o1")
-        for c in range(2):
-            nc.vector.tensor_tensor(o1[:, c * P : (c + 1) * P], sums[c][:], a[:, c * P : (c + 1) * P], ADD)
-        nc.sync.dma_start(out[P : 2 * P, :], o1[:])
+        gc = [fetch(g[0], "gc0")]
+        gc.append(fetch(g[1], "gc1"))
+        s = [product(quantize(c20, "s0"), "s0")]
+        t = [[scaled(0, 0, "g1_codes")]]
+        s.append(product(quantize(c21, "s1"), "s1"))
+        t[0].append(scaled(0, 1, "h_codes"))
+        sc = [fetch(s[0], "sc0")]
+        t.append([scaled(1, 0, "s0")])
+        sc.append(fetch(s[1], "sc1"))
+        t[1].append(scaled(1, 1, "s1"))
+        t[1].append(scaled(1, 2))
+        t[0].append(scaled(0, D - 1, "h1"))
+        sums = [total.tile([P, V], F32, name="sum") for m in range(2)]
+        for m in range(2):
+            a = []
+            for d in range(D - 1):
+                u = banks.tile([P, S], F32, name="bank")
+                first, second = (sc[m], t[m][d]) if (m, d) == (1, 1) else (t[m][d], sc[m])
+                turn(u, first, True, False)
+                turn(u, second, False, True)
+                a.append(keep.tile([P, V], F32, name="a%d%d" % (m, d)))
+                nc.scalar.activation(a[d][:], u[:, 0:V], SILU)
+            for d in range(D - 1):
+                turn(sums[m], a[d], d == 0, d == D - 2)
+        act = {}
+        for m in (1, 0):
+            pre = keep.tile([P, V], F32, name="pre%d" % m)
+            nc.vector.tensor_tensor(pre[:], t[m][D - 1][:], sc[m][:], ADD)
+            act[m] = keep.tile([P, V], F32, name="act%d" % m)
+            nc.scalar.activation(act[m][:], pre[:], SILU)
+        for m in (1, 0):
+            o = keep.tile([P, V], F32, name="o%d" % m)
+            nc.vector.tensor_tensor(o[:], sums[m][:], act[m][:], ADD)
+            nc.sync.dma_start(out[m * P : (m + 1) * P, :], o[:])

@@ -48,7 +48,7 @@ def tile_picked_filmg_silu_p_kernel(
             )
 
         def load_w(w, lo, hi, name):
-            t = keep.tile([P, PACK, hi - lo], F32, name=name)
+            t = keep.tile([P, PACK, hi - lo], F32, name=name, tag=name, align_bytes=64)
             nc.sync.dma_start(t[:], w[:, lo:hi].rearrange("(p j) n -> p j n", j=PACK))
             return t
 
@@ -83,53 +83,47 @@ def tile_picked_filmg_silu_p_kernel(
             )
             return codes[:], scales[:]
 
-        def pick(window, dtype, half, name, tag=None):
-            t = keep.tile([P, HALF], dtype, name=name, tag=tag or name, align_bytes=64)
-            cols = HALF // 16
-            nc.vector.tensor_copy(t[:], window.indirect(offs_t[:, half * cols : (half + 1) * cols]))
-            return t
-
-        xq_w = [pick(xw[:].bitcast(U32), U32, 0, "xq_w0")]
-        xq_s = [pick(xs[:], U8, 0, "xq_s0"), pick(xs[:], U8, 1, "xq_s1")]
-        q10 = quantize(cast(w1_raw[0][:], "c10", False, "shared"), "g0")
-        xq_w.append(pick(xw[:].bitcast(U32), U32, 1, "xq_w1", "shared"))
-
-        def multiply(acc, q, half):
-            nc.tensor.matmul_mx(
-                out=acc, lhsT=q[0].bitcast(FP8X4), lhsT_scale=q[1],
-                rhs=xq_w[half][:].bitcast(FP8X4), rhs_scale=xq_s[half][:], start=True, stop=True,
-            )
+        xq_w = keep.tile([P, S], U32, name="xq_w", align_bytes=64)
+        nc.vector.tensor_copy(xq_w[:], xw[:].bitcast(U32).indirect(offs_t[:]))
+        xq_s = keep.tile([P, S], U8, name="xq_s", align_bytes=64)
+        nc.vector.tensor_copy(xq_s[:], xs[:].indirect(offs_t[:]))
 
         def product(q, name):
             acc = banks.tile([P, S], F32, name="bank")
-            for half in range(2):
-                multiply(acc[:, half * HALF : (half + 1) * HALF], q, half)
+            nc.tensor.matmul_mx(
+                out=acc[:], lhsT=q[0].bitcast(FP8X4), lhsT_scale=q[1],
+                rhs=xq_w[:].bitcast(FP8X4), rhs_scale=xq_s[:], start=True, stop=True,
+            )
             res = keep.tile([P, S], F32, name=name, tag=name, align_bytes=64)
             nc.scalar.copy(res[:], acc[:])
             return res
 
+        c10 = cast(w1_raw[0][:], "c10", False)
         c11 = cast(w1_raw[1][:], "c11", False)
-        g0 = keep.tile([P, S], F32, name="g0")
-        for half in range(2):
-            acc = banks.tile([P, S], F32, name="bank")
-            multiply(acc[:, 0:HALF], q10, half)
-            nc.scalar.copy(g0[:, half * HALF : (half + 1) * HALF], acc[:, 0:HALF])
+        c31 = cast(w3_raw[:, :, P:N], "c31", False)
+        g = [product(quantize(c10, "g0"), "g0")]
+        c30 = cast(w3_raw[:, :, 0:P], "c30", True)
         q11 = quantize(c11, "g1")
-        q3 = quantize(cast(w3_raw[:], "c3", True), "h")
-        g = [g0, product(q11, "g1")]
-        c20 = cast(w2_raw[:, :, 0:P], "c20", False, "g1_codes")
-        h = [product([x[:, 0:P] for x in q3], "h0")]
-        h.append(product([x[:, P:N] for x in q3], "h1"))
-        c21 = cast(w2_raw[:, :, P:N], "c21", False, "h_codes")
+        q30 = quantize(c30, "h0")
+        c2 = cast(w2_raw[:], "c2", True)
+        q31 = quantize(c31, "h1")
+        q2 = quantize(c2, "s")
+        g.append(product(q11, "g1"))
+        h = [product(q30, "h0")]
+        s = [product([x[:, 0:P] for x in q2], "s0")]
+        h.append(product(q31, "h1"))
+        s.append(product([x[:, P:N] for x in q2], "s1"))
 
-        def fetch(res, name):
-            t = keep.tile([P, V], F32, name=name)
+        def fetch(res, name, tag=None):
+            t = keep.tile([P, V], F32, name=name, tag=tag or name, align_bytes=64)
             nc.vector.tensor_copy(t[:], res[:].indirect(cen_t[:]))
             return t
 
-        def scaled(m, d, tag=None):
-            t = keep.tile([P, V], F32, name="t%d%d" % (m, d), tag=tag or "t%d%d" % (m, d), align_bytes=64)
-            nc.vector.tensor_tensor(t[:], h[m][:].indirect(pos_t[d][:]), gc[m][:], MULT)
+        def new(name, tag):
+            return keep.tile([P, V], F32, name=name, tag=tag, align_bytes=64)[:]
+
+        def scaled(m, d, t):
+            nc.vector.tensor_tensor(t, h[m][:].indirect(pos_t[d][:]), gc[m][:], MULT)
             return t
 
         def turn(dst, src, start, stop):
@@ -139,26 +133,21 @@ def tile_picked_filmg_silu_p_kernel(
                     start=start and c == 0, stop=stop and c == 1, is_transpose=True,
                 )
 
-        gc = [fetch(g[0], "gc0")]
-        gc.append(fetch(g[1], "gc1"))
-        s = [product(quantize(c20, "s0"), "s0")]
-        t = [[scaled(0, 0, "g1_codes")]]
-        s.append(product(quantize(c21, "s1"), "s1"))
-        t[0].append(scaled(0, 1, "h_codes"))
+        gc = [fetch(g[0], "gc0", "w2_raw"), fetch(g[1], "gc1", "c2")]
+        t = [[scaled(0, 0, new("t00", "t00"))]]
         sc = [fetch(s[0], "sc0")]
-        t.append([scaled(1, 0, "s0")])
+        t[0].append(scaled(0, 1, new("t01", "s0")))
         sc.append(fetch(s[1], "sc1"))
-        t[1].append(scaled(1, 1, "s1"))
-        t[1].append(scaled(1, 2))
-        t[0].append(scaled(0, D - 1, "h1"))
+        t1 = keep.tile([P, D, V], F32, name="t1", tag="s1", align_bytes=64)
+        t.append([scaled(1, d, t1[:, d, :]) for d in range(D)])
+        t[0].append(scaled(0, D - 1, new("t02", "h1")))
         sums = [total.tile([P, V], F32, name="sum") for m in range(2)]
         for m in range(2):
             a = []
             for d in range(D - 1):
                 u = banks.tile([P, S], F32, name="bank")
-                first, second = (sc[m], t[m][d]) if (m, d) == (1, 1) else (t[m][d], sc[m])
-                turn(u, first, True, False)
-                turn(u, second, False, True)
+                turn(u, sc[m], True, False)
+                turn(u, t[m][d], False, True)
                 a.append(keep.tile([P, V], F32, name="a%d%d" % (m, d)))
                 nc.scalar.activation(a[d][:], u[:, 0:V], SILU)
             for d in range(D - 1):
@@ -166,7 +155,7 @@ def tile_picked_filmg_silu_p_kernel(
         act = {}
         for m in (1, 0):
             pre = keep.tile([P, V], F32, name="pre%d" % m)
-            nc.vector.tensor_tensor(pre[:], t[m][D - 1][:], sc[m][:], ADD)
+            nc.vector.tensor_tensor(pre[:], t[m][D - 1], sc[m][:], ADD)
             act[m] = keep.tile([P, V], F32, name="act%d" % m)
             nc.scalar.activation(act[m][:], pre[:], SILU)
         for m in (1, 0):

@@ -52,7 +52,7 @@ def tile_picked_filmg_silu_p_kernel(
             nc.sync.dma_start(t[:], w[:, lo:hi].rearrange("(p j) n -> p j n", j=PACK))
             return t
 
-        w1_raw = [load_w(w1, 0, P, "w1_raw0"), load_w(w1, P, N, "w1_raw1")]
+        w1_raw = load_w(w1, 0, N, "w1_raw")
         w3_raw = load_w(w3, 0, N, "w3_raw")
         w2_raw = load_w(w2, 0, N, "w2_raw")
         cen_t = load_list(cen, "cen_t")
@@ -98,8 +98,8 @@ def tile_picked_filmg_silu_p_kernel(
             nc.scalar.copy(res[:], acc[:])
             return res
 
-        c10 = cast(w1_raw[0][:], "c10", False)
-        c11 = cast(w1_raw[1][:], "c11", False)
+        c10 = cast(w1_raw[:, :, 0:P], "c10", False)
+        c11 = cast(w1_raw[:, :, P:N], "c11", False)
         c31 = cast(w3_raw[:, :, P:N], "c31", False)
         g = [product(quantize(c10, "g0"), "g0")]
         c30 = cast(w3_raw[:, :, 0:P], "c30", True)
@@ -134,15 +134,19 @@ def tile_picked_filmg_silu_p_kernel(
                 )
 
         gc = [fetch(g[0], "gc0", "w2_raw"), fetch(g[1], "gc1", "c2")]
-        t = [[scaled(0, 0, new("t00", "t00"))]]
+        t00 = scaled(0, 0, new("t00", "t00"))
+        t02 = scaled(0, D - 1, new("t02", "t02"))
         sc = [fetch(s[0], "sc0")]
-        t[0].append(scaled(0, 1, new("t01", "s0")))
+        t = [[t00, scaled(0, 1, new("t01", "s0")), t02]]
         sc.append(fetch(s[1], "sc1"))
         t1 = keep.tile([P, D, V], F32, name="t1", tag="s1", align_bytes=64)
-        t.append([scaled(1, d, t1[:, d, :]) for d in range(D)])
-        t[0].append(scaled(0, D - 1, new("t02", "h1")))
         sums = [total.tile([P, V], F32, name="sum") for m in range(2)]
+        act = []
         for m in range(2):
+            if m == 1:
+                t.append([scaled(1, d, t1[:, d, :]) for d in range(D)])
+            pre = keep.tile([P, V], F32, name="pre%d" % m)
+            nc.vector.tensor_tensor(pre[:], t[m][D - 1], sc[m][:], ADD)
             a = []
             for d in range(D - 1):
                 u = banks.tile([P, S], F32, name="bank")
@@ -150,15 +154,11 @@ def tile_picked_filmg_silu_p_kernel(
                 turn(u, t[m][d], False, True)
                 a.append(keep.tile([P, V], F32, name="a%d%d" % (m, d)))
                 nc.scalar.activation(a[d][:], u[:, 0:V], SILU)
+            act.append(keep.tile([P, V], F32, name="act%d" % m))
+            nc.scalar.activation(act[m][:], pre[:], SILU)
             for d in range(D - 1):
                 turn(sums[m], a[d], d == 0, d == D - 2)
-        act = {}
-        for m in (1, 0):
-            pre = keep.tile([P, V], F32, name="pre%d" % m)
-            nc.vector.tensor_tensor(pre[:], t[m][D - 1], sc[m][:], ADD)
-            act[m] = keep.tile([P, V], F32, name="act%d" % m)
-            nc.scalar.activation(act[m][:], pre[:], SILU)
-        for m in (1, 0):
+        for m in range(2):
             o = keep.tile([P, V], F32, name="o%d" % m)
             nc.vector.tensor_tensor(o[:], sums[m][:], act[m][:], ADD)
             nc.sync.dma_start(out[m * P : (m + 1) * P, :], o[:])

@@ -20,6 +20,7 @@ FP8X4 = mybir.dt.float8_e4m3fn_x4
 MULT = mybir.AluOpType.mult
 ADD = mybir.AluOpType.add
 SILU = mybir.ActivationFunctionType.Silu
+COPY = mybir.ActivationFunctionType.Copy
 
 
 def tile_picked_filmg_silu_p_kernel(
@@ -28,103 +29,88 @@ def tile_picked_filmg_silu_p_kernel(
     nc = tc.nc
     with ExitStack() as ctx:
         keep = ctx.enter_context(tc.tile_pool(name="keep", bufs=1))
-        banks = ctx.enter_context(tc.psum_pool(name="banks", bufs=6))
-        total = ctx.enter_context(tc.psum_pool(name="total", bufs=2))
+        banks = ctx.enter_context(tc.psum_pool(name="banks", bufs=1))
+
+        def new(name, width, dtype=F32, tag=None):
+            return keep.tile([P, width], dtype, name=name, tag=tag or name, align_bytes=64)[:]
 
         def load_list(src, name):
             t = keep.tile(list(src.shape), U16, name=name)
             nc.sync.dma_start(t[:], src)
             return t
 
-        offs_t = load_list(offs, "offs_t")
-
-        xw = keep.tile([P, T], I32, name="xw", align_bytes=64)
-        nc.scalar.dma_start(xw[:], x_words[0].rearrange("p n t -> p (n t)").bitcast(I32))
-        xs = keep.tile([P, T], U8, name="xs", align_bytes=64)
-        nc.vector.memset(xs[:].bitcast(I32), 0)
-        for q in range(4):
-            nc.sync.dma_start(
-                xs[32 * q : 32 * q + 4, :].bitcast(I32), x_scales[0, 4 * q : 4 * q + 4, :].bitcast(I32)
-            )
-
-        def load_w(w, lo, hi, name):
-            t = keep.tile([P, PACK, hi - lo], F32, name=name, tag=name, align_bytes=64)
-            nc.sync.dma_start(t[:], w[:, lo:hi].rearrange("(p j) n -> p j n", j=PACK))
+        def load_w(w, name, eng=nc.sync):
+            t = keep.tile([P, PACK, N], F32, name=name, tag=name, align_bytes=64)
+            eng.dma_start(t[:], w.rearrange("(p j) n -> p j n", j=PACK))
             return t
 
-        w1_raw = load_w(w1, 0, N, "w1_raw")
-        w3_raw = load_w(w3, 0, N, "w3_raw")
-        w2_raw = load_w(w2, 0, N, "w2_raw")
-        cen_t = load_list(cen, "cen_t")
-        pos_t = [load_list(pos1, "pos1_t"), load_list(pos2, "pos2_t"), load_list(pos3, "pos3_t")]
-
-        warm = keep.tile([P, 8], F32, name="warm")
-        nc.vector.memset(warm[:, 0:1], 0.0)
-        nc.scalar.activation(warm[:, 4:5], warm[:, 0:1], SILU)
-
-        ident = keep.tile([P, P], F32, name="ident")
-        make_identity(nc, ident[:])
-
-        def cast(raw, name, on_vector, tag=None):
+        def cast(raw, name, eng, tag=None):
             t = keep.tile([P, raw.shape[2], PACK], BF16, name=name, tag=tag or name, align_bytes=64)
             dst = t[:].rearrange("p (c i) j -> p c j i", i=4)
             src = raw.rearrange("p j (c i) -> p c j i", i=4)
-            if on_vector:
+            if eng == "v":
+                nc.vector.tensor_copy(dst, src)
+            elif eng == "s":
+                nc.scalar.copy(dst, src)
+            else:
+                nc.gpsimd.tensor_scalar(dst, src, 1.0, 0.0, MULT, ADD)
+            return t
+
+        def quantize(grouped, name, tag=None):
+            codes = new(name + "_codes", grouped.shape[1], U32, tag)
+            scales = new(name + "_scales", grouped.shape[1], U8)
+            nc.vector.quantize_mx(
+                out=codes.bitcast(FP8X4), scales=scales, in_=grouped[:].rearrange("p c j -> p (c j)")
+            )
+            return codes, scales
+
+        def bank(tag):
+            return banks.tile([P, S], F32, name=tag, tag=tag)
+
+        def product(q, tag, lo=0, halves=(0, 1)):
+            acc = bank(tag)
+            for i in halves:
+                nc.tensor.matmul_mx(
+                    out=acc[:, i * HALF : (i + 1) * HALF],
+                    lhsT=q[0][:, lo : lo + P].bitcast(FP8X4), lhsT_scale=q[1][:, lo : lo + P],
+                    rhs=xq_w[:, i * HALF : (i + 1) * HALF].bitcast(FP8X4), rhs_scale=xq_s[:, i * HALF : (i + 1) * HALF],
+                    start=True, stop=True,
+                )
+            return acc
+
+        def whole(q, tag, lo=0):
+            acc = bank(tag)
+            nc.tensor.matmul_mx(
+                out=acc[:], lhsT=q[0][:, lo : lo + P].bitcast(FP8X4), lhsT_scale=q[1][:, lo : lo + P],
+                rhs=xq_w.bitcast(FP8X4), rhs_scale=xq_s, start=True, stop=True,
+            )
+            return acc
+
+        def move(dst, src, eng):
+            if eng == "v":
                 nc.vector.tensor_copy(dst, src)
             else:
                 nc.scalar.copy(dst, src)
-            return t
 
-        def quantize(grouped, name):
-            codes = keep.tile([P, grouped.shape[1]], U32, name=name + "_codes", tag=name + "_codes", align_bytes=64)
-            scales = keep.tile([P, grouped.shape[1]], U8, name=name + "_scales", align_bytes=64)
-            nc.vector.quantize_mx(
-                out=codes[:].bitcast(FP8X4), scales=scales[:], in_=grouped[:].rearrange("p c j -> p (c j)")
-            )
-            return codes[:], scales[:]
-
-        xq_w = keep.tile([P, S], U32, name="xq_w", align_bytes=64)
-        nc.vector.tensor_copy(xq_w[:], xw[:].bitcast(U32).indirect(offs_t[:]))
-        xq_s = keep.tile([P, S], U8, name="xq_s", align_bytes=64)
-        nc.vector.tensor_copy(xq_s[:], xs[:].indirect(offs_t[:]))
-
-        def product(q, name):
-            acc = banks.tile([P, S], F32, name="bank")
-            nc.tensor.matmul_mx(
-                out=acc[:], lhsT=q[0].bitcast(FP8X4), lhsT_scale=q[1],
-                rhs=xq_w[:].bitcast(FP8X4), rhs_scale=xq_s[:], start=True, stop=True,
-            )
-            res = keep.tile([P, S], F32, name=name, tag=name, align_bytes=64)
-            nc.scalar.copy(res[:], acc[:])
+        def empty(acc, name, eng, tag=None):
+            res = new(name, S, F32, tag)
+            if eng == "v":
+                nc.vector.tensor_copy(res, acc[:])
+            else:
+                nc.scalar.copy(res, acc[:])
             return res
 
-        c10 = cast(w1_raw[:, :, 0:P], "c10", False)
-        c11 = cast(w1_raw[:, :, P:N], "c11", False)
-        c31 = cast(w3_raw[:, :, P:N], "c31", False)
-        g = [product(quantize(c10, "g0"), "g0")]
-        c30 = cast(w3_raw[:, :, 0:P], "c30", True)
-        q11 = quantize(c11, "g1")
-        q30 = quantize(c30, "h0")
-        c2 = cast(w2_raw[:], "c2", True)
-        q31 = quantize(c31, "h1")
-        q2 = quantize(c2, "s")
-        g.append(product(q11, "g1"))
-        h = [product(q30, "h0")]
-        s = [product([x[:, 0:P] for x in q2], "s0")]
-        h.append(product(q31, "h1"))
-        s.append(product([x[:, P:N] for x in q2], "s1"))
-
-        def fetch(res, name, tag=None):
-            t = keep.tile([P, V], F32, name=name, tag=tag or name, align_bytes=64)
-            nc.vector.tensor_copy(t[:], res[:].indirect(cen_t[:]))
+        def fetch(res, name, eng, tag=None):
+            t = new(name, V, F32, tag)
+            if eng == "v":
+                nc.vector.tensor_copy(t, res.indirect(cen_t[:]))
+            else:
+                nc.scalar.activation(t, res.indirect(cen_t[:]), COPY)
             return t
 
-        def new(name, tag):
-            return keep.tile([P, V], F32, name=name, tag=tag, align_bytes=64)[:]
-
-        def scaled(m, d, t):
-            nc.vector.tensor_tensor(t, h[m][:].indirect(pos_t[d][:]), gc[m][:], MULT)
-            return t
+        def scaled(h, gc, t):
+            for d in range(D):
+                nc.vector.tensor_tensor(t[d], h.indirect(pos_t[d][:]), gc, MULT)
 
         def turn(dst, src, start, stop):
             for c in range(2):
@@ -133,32 +119,89 @@ def tile_picked_filmg_silu_p_kernel(
                     start=start and c == 0, stop=stop and c == 1, is_transpose=True,
                 )
 
-        gc = [fetch(g[0], "gc0", "w2_raw"), fetch(g[1], "gc1", "c2")]
-        t00 = scaled(0, 0, new("t00", "t00"))
-        t02 = scaled(0, D - 1, new("t02", "t02"))
-        sc = [fetch(s[0], "sc0")]
-        t = [[t00, scaled(0, 1, new("t01", "s0")), t02]]
-        sc.append(fetch(s[1], "sc1"))
-        t1 = keep.tile([P, D, V], F32, name="t1", tag="s1", align_bytes=64)
-        sums = [total.tile([P, V], F32, name="sum") for m in range(2)]
-        act = []
+        def silu(src, name, tag=None):
+            t = new(name, src.shape[1], F32, tag)
+            nc.scalar.activation(t, src, SILU)
+            return t
+
+        def add(a, b, name, tag=None):
+            t = new(name, a.shape[1], F32, tag)
+            nc.vector.tensor_tensor(t, a, b, ADD)
+            return t
+
+        xs = new("xs", T, U8)
+        offs_t = load_list(offs, "offs_t")
+        for q in range(4):
+            rows = x_scales[0, 4 * q : 4 * q + 4, :].bitcast(I32)
+            eng = nc.scalar if q % 2 == 0 else nc.sync
+            eng.dma_start(xs[32 * q : 32 * q + 32, :].bitcast(I32), rows.unsqueeze(0).to_broadcast([8, 4, T // 4]))
+        w1_raw = load_w(w1, "w1_raw")
+        xw = new("xw", T, I32)
+        nc.sync.dma_start(xw, x_words[0].rearrange("p n t -> p (n t)").bitcast(I32))
+        w3_raw = load_w(w3, "w3_raw")
+        cen_t = load_list(cen, "cen_t")
+        pos_t = [load_list(pos1, "pos1_t"), load_list(pos2, "pos2_t"), load_list(pos3, "pos3_t")]
+        w2_raw = load_w(w2, "w2_raw")
+
+        warm = keep.tile([P, 8], F32, name="warm")
+        nc.vector.memset(warm[:, 0:1], 0.0)
+        nc.scalar.activation(warm[:, 4:5], warm[:, 0:1], SILU)
+
+        ident = keep.tile([P, P], F32, name="ident")
+        make_identity(nc, ident[:])
+
+        xq_s = new("xq_s", S, U8)
+        nc.vector.tensor_copy(xq_s, xs.indirect(offs_t[:]))
+        c10 = cast(w1_raw[:, :, 0:P], "c10", "v")
+        c11 = cast(w1_raw[:, :, P:N], "c11", "s")
+        q10 = quantize(c10, "g0")
+        q11 = quantize(c11, "g1")
+        xq_w = new("xq_w", S, U32)
+        g0 = new("g0", S)
+        g1 = new("g1", S)
+        nc.vector.tensor_copy(xq_w[:, 0:HALF], xw.bitcast(U32).indirect(offs_t[:, 0:16]))
+        pg0a = product(q10, "b0", 0, (0,))
+        pg1a = product(q11, "b1", 0, (0,))
+        nc.vector.tensor_copy(xq_w[:, HALF:S], xw.bitcast(U32).indirect(offs_t[:, 16:32]))
+        pg0b = product(q10, "b2", 0, (1,))
+        pg1b = product(q11, "b3", 0, (1,))
+        move(g0[:, 0:HALF], pg0a[:, 0:HALF], "s")
+        move(g1[:, 0:HALF], pg1a[:, 0:HALF], "s")
+        move(g0[:, HALF:S], pg0b[:, HALF:S], "s")
+        move(g1[:, HALF:S], pg1b[:, HALF:S], "s")
+        c30 = cast(w3_raw[:, :, 0:P], "c30", "v")
+        c31 = cast(w3_raw[:, :, P:N], "c31", "v")
+        ph0 = whole(quantize(c30, "h0", "h0_codes"), "b4")
+        ph1 = whole(quantize(c31, "h1"), "b5")
+        gc0 = fetch(g0, "gc0", "s")
+        h0 = empty(ph0, "h0", "s")
+        gc1 = fetch(g1, "gc1", "s", "h0_codes")
+        c20 = cast(w2_raw[:, :, 0:P], "c20", "v")
+        c21 = cast(w2_raw[:, :, P:N], "c21", "v")
+        ps0 = whole(quantize(c20, "s0"), "b6")
+        ps1 = whole(quantize(c21, "s1"), "b7")
+        h1 = empty(ph1, "h1", "v", "c20")
+        s0 = empty(ps0, "s0", "s")
+        s1 = empty(ps1, "s1", "s")
+        tt = keep.tile([P, 2 * D, V], F32, name="tt", tag="w2_raw", align_bytes=64)
+        t = [[tt[:, m * D + d, :] for d in range(D)] for m in range(2)]
+        scaled(h0, gc0, t[0])
+        sc = [fetch(s0, "sc0", "s"), fetch(s1, "sc1", "s")]
+        scaled(h1, gc1, t[1])
+        a = []
         for m in range(2):
-            if m == 1:
-                t.append([scaled(1, d, t1[:, d, :]) for d in range(D)])
-            pre = keep.tile([P, V], F32, name="pre%d" % m)
-            nc.vector.tensor_tensor(pre[:], t[m][D - 1], sc[m][:], ADD)
-            a = []
             for d in range(D - 1):
-                u = banks.tile([P, S], F32, name="bank")
-                turn(u, sc[m], True, False)
-                turn(u, t[m][d], False, True)
-                a.append(keep.tile([P, V], F32, name="a%d%d" % (m, d)))
-                nc.scalar.activation(a[d][:], u[:, 0:V], SILU)
-            act.append(keep.tile([P, V], F32, name="act%d" % m))
-            nc.scalar.activation(act[m][:], pre[:], SILU)
-            for d in range(D - 1):
-                turn(sums[m], a[d], d == 0, d == D - 2)
+                u = bank("b%d" % (2 * m + d))
+                first, second = (t[m][d], sc[m]) if m == 0 else (sc[m], t[m][d])
+                turn(u, first, True, False)
+                turn(u, second, False, True)
+                a.append(silu(u[:, 0:V], "a%d%d" % (m, d)))
+        pre = [add(t[m][D - 1], sc[m], "pre%d" % m) for m in range(2)]
+        act = [t[1][1], pre[0]]
         for m in range(2):
-            o = keep.tile([P, V], F32, name="o%d" % m)
-            nc.vector.tensor_tensor(o[:], sums[m][:], act[m][:], ADD)
-            nc.sync.dma_start(out[m * P : (m + 1) * P, :], o[:])
+            nc.scalar.activation(act[m], pre[m], SILU)
+            sums = bank("b%d" % (4 + m))[:, 0:V]
+            for d in range(D - 1):
+                turn(sums, a[2 * m + d], d == 0, d == D - 2)
+            o = add(sums, act[m], "o%d" % m)
+            nc.sync.dma_start(out[m * P : (m + 1) * P, :], o)

@@ -187,21 +187,38 @@ def tile_picked_filmg_silu_p_kernel(
         t = [[tt[:, m * D + d, :] for d in range(D)] for m in range(2)]
         scaled(h0, gc0, t[0])
         sc = [fetch(s0, "sc0", "s"), fetch(s1, "sc1", "s")]
-        scaled(h1, gc1, t[1])
-        a = []
-        for m in range(2):
-            for d in range(D - 1):
-                u = bank("b%d" % (2 * m + d))
-                first, second = (t[m][d], sc[m]) if m == 0 else (sc[m], t[m][d])
-                turn(u, first, True, False)
-                turn(u, second, False, True)
-                a.append(silu(u[:, 0:V], "a%d%d" % (m, d)))
-        pre = [add(t[m][D - 1], sc[m], "pre%d" % m) for m in range(2)]
-        act = [t[1][1], pre[0]]
-        for m in range(2):
-            nc.scalar.activation(act[m], pre[m], SILU)
-            sums = bank("b%d" % (4 + m))[:, 0:V]
-            for d in range(D - 1):
-                turn(sums, a[2 * m + d], d == 0, d == D - 2)
-            o = add(sums, act[m], "o%d" % m)
-            nc.sync.dma_start(out[m * P : (m + 1) * P, :], o)
+        for d in range(D - 1):
+            nc.vector.tensor_tensor(t[1][d], h1.indirect(pos_t[d][:]), gc1, MULT)
+        cols = [slice(c * P, (c + 1) * P) for c in range(2)]
+        for c in range(2):
+            nc.vector.tensor_tensor(
+                t[1][D - 1][:, cols[c]], h1.indirect(pos_t[D - 1][:, 8 * c : 8 * c + 8]), gc1[:, cols[c]], MULT
+            )
+        def through(m, d, tag):
+            u = bank(tag)
+            first, second = (t[m][d], sc[m]) if m == 0 else (sc[m], t[m][d])
+            turn(u, first, True, False)
+            turn(u, second, False, True)
+            return silu(u[:, 0:V], "a%d%d" % (m, d))
+
+        a0 = [through(0, d, "b%d" % d) for d in range(D)]
+        a1 = [through(1, d, "b%d" % (D + d)) for d in range(D - 1)]
+        sum0 = bank("b5")[:, 0:V]
+        for d in range(D):
+            turn(sum0, a0[d], d == 0, d == D - 1)
+        o0 = new("o0", V)
+        nc.vector.tensor_copy(o0, sum0)
+        nc.sync.dma_start(out[0:P, :], o0)
+        pre = new("pre", V)
+        act = [t[1][1][:, cols[1]], pre[:, cols[0]]]
+        for c in range(2):
+            nc.vector.tensor_tensor(pre[:, cols[c]], t[1][D - 1][:, cols[c]], sc[1][:, cols[c]], ADD)
+        for c in range(2):
+            nc.scalar.activation(act[c], pre[:, cols[c]], SILU)
+        sum1 = bank("b6")[:, 0:V]
+        for d in range(D - 1):
+            turn(sum1, a1[d], d == 0, d == D - 2)
+        o1 = new("o1", V)
+        for c in range(2):
+            nc.vector.tensor_tensor(o1[:, cols[c]], sum1[:, cols[c]], act[c], ADD)
+        nc.sync.dma_start(out[P:N, :], o1)

@@ -178,10 +178,14 @@ def tile_picked_filmg_silu_p_kernel(
         gc1 = fetch(g1, "gc1", "s", "h0_codes")
         c20 = cast(w2_raw[:, :, 0:P], "c20", "v")
         c21 = cast(w2_raw[:, :, P:N], "c21", "v")
-        ps0 = whole(quantize(c20, "s0"), "b6")
-        ps1 = whole(quantize(c21, "s1"), "b7")
+        q20 = quantize(c20, "s0")
+        q21 = quantize(c21, "s1")
+        ps0 = whole(q20, "b6")
+        ps1 = whole(q21, "b7")
         h1 = empty(ph1, "h1", "v", "c20")
         s0 = empty(ps0, "s0", "s")
+        whole(q20, "b6")
+        product(q21, "b6", 0, (0,))
         s1 = empty(ps1, "s1", "s")
         tt = keep.tile([P, 2 * D, V], F32, name="tt", tag="w2_raw", align_bytes=64)
         t = [[tt[:, m * D + d, :] for d in range(D)] for m in range(2)]

@@ -175,7 +175,6 @@ def tile_picked_filmg_silu_p_kernel(
         ph1 = whole(quantize(c31, "h1"), "b5")
         gc0 = fetch(g0, "gc0", "s")
         h0 = empty(ph0, "h0", "s")
-        gc1 = fetch(g1, "gc1", "s", "h0_codes")
         c20 = cast(w2_raw[:, :, 0:P], "c20", "v")
         c21 = cast(w2_raw[:, :, P:N], "c21", "v")
         q20 = quantize(c20, "s0")
@@ -183,21 +182,30 @@ def tile_picked_filmg_silu_p_kernel(
         ps0 = whole(q20, "b6")
         ps1 = whole(q21, "b7")
         h1 = empty(ph1, "h1", "v", "c20")
+        tt = keep.tile([P, 2 * D + 1, V], F32, name="tt", tag="w2_raw", align_bytes=64)
+        nc.scalar.activation(tt[:, 2 * D, P:V], g1.indirect(cen_t[:, 8:16]), COPY)
         s0 = empty(ps0, "s0", "s")
         whole(q20, "b6")
         product(q21, "b6", 0, (0,))
         s1 = empty(ps1, "s1", "s")
-        tt = keep.tile([P, 2 * D, V], F32, name="tt", tag="w2_raw", align_bytes=64)
         t = [[tt[:, m * D + d, :] for d in range(D)] for m in range(2)]
-        scaled(h0, gc0, t[0])
+        gc1 = tt[:, 2 * D, :]
+        for d in range(D):
+            if d == D - 1:
+                nc.vector.tensor_copy(gc1[:, 0:P], g1.indirect(cen_t[:, 0:8]))
+            nc.vector.tensor_tensor(t[0][d], h0.indirect(pos_t[d][:]), gc0, MULT)
         sc = [fetch(s0, "sc0", "s"), fetch(s1, "sc1", "s")]
-        for d in range(D - 1):
-            nc.vector.tensor_tensor(t[1][d], h1.indirect(pos_t[d][:]), gc1, MULT)
         cols = [slice(c * P, (c + 1) * P) for c in range(2)]
-        for c in range(2):
-            nc.vector.tensor_tensor(
-                t[1][D - 1][:, cols[c]], h1.indirect(pos_t[D - 1][:, 8 * c : 8 * c + 8]), gc1[:, cols[c]], MULT
-            )
+        nc.vector.tensor_tensor(t[1][0], h1.indirect(pos_t[0][:]), gc1, MULT)
+        for d in range(1, D):
+            for c in range(2):
+                nc.vector.tensor_tensor(
+                    t[1][d][:, cols[c]], h1.indirect(pos_t[d][:, 8 * c : 8 * c + 8]), gc1[:, cols[c]], MULT
+                )
+
+        def flip(dst, src, start, stop):
+            nc.tensor.matmul(dst, src, ident[:], start=start, stop=stop, is_transpose=True)
+
         def through(m, d, tag):
             u = bank(tag)
             first, second = (t[m][d], sc[m]) if m == 0 else (sc[m], t[m][d])
@@ -206,23 +214,30 @@ def tile_picked_filmg_silu_p_kernel(
             return silu(u[:, 0:V], "a%d%d" % (m, d))
 
         a0 = [through(0, d, "b%d" % d) for d in range(D)]
-        a1 = [through(1, d, "b%d" % (D + d)) for d in range(D - 1)]
-        sum0 = bank("b5")[:, 0:V]
+        a10 = through(1, 0, "b3")
+        a11 = []
+        for c in range(2):
+            u = bank("b%d" % (4 + c))[:, 0:P]
+            flip(u, sc[1][:, cols[c]], True, False)
+            flip(u, t[1][1][:, cols[c]], False, True)
+            a11.append(silu(u, "a11%d" % c))
+        sum0 = bank("b0")[:, 0:V]
         for d in range(D):
             turn(sum0, a0[d], d == 0, d == D - 1)
         o0 = new("o0", V)
         nc.vector.tensor_copy(o0, sum0)
         nc.sync.dma_start(out[0:P, :], o0)
         pre = new("pre", V)
-        act = [t[1][1][:, cols[1]], pre[:, cols[0]]]
+        act = [t[1][1][:, cols[1]], a11[0]]
         for c in range(2):
             nc.vector.tensor_tensor(pre[:, cols[c]], t[1][D - 1][:, cols[c]], sc[1][:, cols[c]], ADD)
+        sum1 = [bank("b%d" % (6 + c))[:, 0:P] for c in range(2)]
+        for c in range(2):
+            flip(sum1[c], a10[:, cols[c]], True, False)
+            flip(sum1[c], a11[c], False, True)
         for c in range(2):
             nc.scalar.activation(act[c], pre[:, cols[c]], SILU)
-        sum1 = bank("b6")[:, 0:V]
-        for d in range(D - 1):
-            turn(sum1, a1[d], d == 0, d == D - 2)
         o1 = new("o1", V)
         for c in range(2):
-            nc.vector.tensor_tensor(o1[:, cols[c]], sum1[:, cols[c]], act[c], ADD)
+            nc.vector.tensor_tensor(o1[:, cols[c]], sum1[c], act[c], ADD)
         nc.sync.dma_start(out[P:N, :], o1)

@@ -175,6 +175,7 @@ def tile_picked_filmg_silu_p_kernel(
         ph1 = whole(quantize(c31, "h1"), "b5")
         gc0 = fetch(g0, "gc0", "s")
         h0 = empty(ph0, "h0", "s")
+        gc1 = fetch(g1, "gc1", "s", "h0_codes")
         c20 = cast(w2_raw[:, :, 0:P], "c20", "v")
         c21 = cast(w2_raw[:, :, P:N], "c21", "v")
         q20 = quantize(c20, "s0")
@@ -182,18 +183,13 @@ def tile_picked_filmg_silu_p_kernel(
         ps0 = whole(q20, "b6")
         ps1 = whole(q21, "b7")
         h1 = empty(ph1, "h1", "v", "c20")
-        tt = keep.tile([P, 2 * D + 1, V], F32, name="tt", tag="w2_raw", align_bytes=64)
-        nc.scalar.activation(tt[:, 2 * D, P:V], g1.indirect(cen_t[:, 8:16]), COPY)
         s0 = empty(ps0, "s0", "s")
         whole(q20, "b6")
-        product(q21, "b6", 0, (0,))
         s1 = empty(ps1, "s1", "s")
+        product(q21, "b7", 0, (0,))
+        tt = keep.tile([P, 2 * D, V], F32, name="tt", tag="w2_raw", align_bytes=64)
         t = [[tt[:, m * D + d, :] for d in range(D)] for m in range(2)]
-        gc1 = tt[:, 2 * D, :]
-        for d in range(D):
-            if d == D - 1:
-                nc.vector.tensor_copy(gc1[:, 0:P], g1.indirect(cen_t[:, 0:8]))
-            nc.vector.tensor_tensor(t[0][d], h0.indirect(pos_t[d][:]), gc0, MULT)
+        scaled(h0, gc0, t[0])
         sc = [fetch(s0, "sc0", "s"), fetch(s1, "sc1", "s")]
         cols = [slice(c * P, (c + 1) * P) for c in range(2)]
         nc.vector.tensor_tensor(t[1][0], h1.indirect(pos_t[0][:]), gc1, MULT)
@@ -208,7 +204,7 @@ def tile_picked_filmg_silu_p_kernel(
 
         def through(m, d, tag):
             u = bank(tag)
-            first, second = (t[m][d], sc[m]) if m == 0 else (sc[m], t[m][d])
+            first, second = (t[m][d], sc[m]) if m == 0 and d < D - 1 else (sc[m], t[m][d])
             turn(u, first, True, False)
             turn(u, second, False, True)
             return silu(u[:, 0:V], "a%d%d" % (m, d))

@@ -179,18 +179,18 @@ def tile_picked_filmg_silu_p_kernel(
         c20 = cast(w2_raw[:, :, 0:P], "c20", "v")
         c21 = cast(w2_raw[:, :, P:N], "c21", "v")
         q20 = quantize(c20, "s0")
-        q21 = quantize(c21, "s1")
+        q21 = quantize(c21, "s1", "s1_codes")
         ps0 = whole(q20, "b6")
-        ps1 = whole(q21, "b7")
         h1 = empty(ph1, "h1", "v", "c20")
+        ps1 = whole(q21, "b5")
         s0 = empty(ps0, "s0", "s")
-        whole(q20, "b6")
+        product(q20, "b6", 0, (0,))
         s1 = empty(ps1, "s1", "s")
-        product(q21, "b7", 0, (0,))
+        whole(q20, "b5")
         tt = keep.tile([P, 2 * D, V], F32, name="tt", tag="w2_raw", align_bytes=64)
         t = [[tt[:, m * D + d, :] for d in range(D)] for m in range(2)]
         scaled(h0, gc0, t[0])
-        sc = [fetch(s0, "sc0", "s"), fetch(s1, "sc1", "s")]
+        sc = [fetch(s0, "sc0", "s", "s1_codes"), fetch(s1, "sc1", "s")]
         cols = [slice(c * P, (c + 1) * P) for c in range(2)]
         nc.vector.tensor_tensor(t[1][0], h1.indirect(pos_t[0][:]), gc1, MULT)
         for d in range(1, D):

@@ -224,7 +224,7 @@ def tile_picked_filmg_silu_p_kernel(
         nc.vector.tensor_copy(o0, sum0)
         nc.sync.dma_start(out[0:P, :], o0)
         pre = new("pre", V)
-        act = [t[1][1][:, cols[1]], a11[0]]
+        act = [t[1][1][:, cols[1]], a10[:, cols[0]]]
         for c in range(2):
             nc.vector.tensor_tensor(pre[:, cols[c]], t[1][D - 1][:, cols[c]], sc[1][:, cols[c]], ADD)
         sum1 = [bank("b%d" % (6 + c))[:, 0:P] for c in range(2)]
@@ -236,4 +236,4 @@ def tile_picked_filmg_silu_p_kernel(
         o1 = new("o1", V)
         for c in range(2):
             nc.vector.tensor_tensor(o1[:, cols[c]], sum1[c], act[c], ADD)
-        nc.sync.dma_start(out[P:N, :], o1)
+            nc.sync.dma_start(out[P:N, cols[c]], o1[:, cols[c]])

@@ -40,7 +40,7 @@ def tile_picked_filmg_silu_p_kernel(
             return t
 
         def load_w(w, name, eng=nc.sync):
-            t = keep.tile([P, PACK, N], F32, name=name, tag=name, align_bytes=64)
+            t = keep.tile([P, PACK, w.shape[1]], F32, name=name, tag=name, align_bytes=64)
             eng.dma_start(t[:], w.rearrange("(p j) n -> p j n", j=PACK))
             return t
 
@@ -131,17 +131,21 @@ def tile_picked_filmg_silu_p_kernel(
 
         xs = new("xs", T, U8)
         offs_t = load_list(offs, "offs_t")
+        xs_rows = new("xs_rows", T // 4, I32)
+        nc.vector.memset(xs.bitcast(I32), 0)
         for q in range(4):
-            rows = x_scales[0, 4 * q : 4 * q + 4, :].bitcast(I32)
+            live = slice(32 * q, 32 * q + 4)
             eng = nc.scalar if q % 2 == 0 else nc.sync
-            eng.dma_start(xs[32 * q : 32 * q + 32, :].bitcast(I32), rows.unsqueeze(0).to_broadcast([8, 4, T // 4]))
-        w1_raw = load_w(w1, "w1_raw")
+            eng.dma_start(xs_rows[live, :], x_scales[0, 4 * q : 4 * q + 4, :].bitcast(I32))
+            nc.vector.tensor_copy(xs.bitcast(I32)[live, :], xs_rows[live, :])
+        w1_raw = [load_w(w1[:, 0:P], "w10_raw")]
         xw = new("xw", T, I32)
         nc.sync.dma_start(xw, x_words[0].rearrange("p n t -> p (n t)").bitcast(I32))
+        w1_raw.append(load_w(w1[:, P:N], "w11_raw"))
         w3_raw = load_w(w3, "w3_raw")
         cen_t = load_list(cen, "cen_t")
-        pos_t = [load_list(pos1, "pos1_t"), load_list(pos2, "pos2_t"), load_list(pos3, "pos3_t")]
         w2_raw = load_w(w2, "w2_raw")
+        pos_t = [load_list(pos1, "pos1_t"), load_list(pos2, "pos2_t"), load_list(pos3, "pos3_t")]
 
         warm = keep.tile([P, 8], F32, name="warm")
         nc.vector.memset(warm[:, 0:1], 0.0)
@@ -152,23 +156,20 @@ def tile_picked_filmg_silu_p_kernel(
 
         xq_s = new("xq_s", S, U8)
         nc.vector.tensor_copy(xq_s, xs.indirect(offs_t[:]))
-        c10 = cast(w1_raw[:, :, 0:P], "c10", "v")
-        c11 = cast(w1_raw[:, :, P:N], "c11", "s")
+        c10 = cast(w1_raw[0][:], "c10", "s")
+        c11 = cast(w1_raw[1][:], "c11", "s")
         q10 = quantize(c10, "g0")
-        q11 = quantize(c11, "g1")
         xq_w = new("xq_w", S, U32)
         g0 = new("g0", S)
         g1 = new("g1", S)
-        nc.vector.tensor_copy(xq_w[:, 0:HALF], xw.bitcast(U32).indirect(offs_t[:, 0:16]))
-        pg0a = product(q10, "b0", 0, (0,))
-        pg1a = product(q11, "b1", 0, (0,))
-        nc.vector.tensor_copy(xq_w[:, HALF:S], xw.bitcast(U32).indirect(offs_t[:, 16:32]))
-        pg0b = product(q10, "b2", 0, (1,))
-        pg1b = product(q11, "b3", 0, (1,))
-        move(g0[:, 0:HALF], pg0a[:, 0:HALF], "s")
-        move(g1[:, 0:HALF], pg1a[:, 0:HALF], "s")
-        move(g0[:, HALF:S], pg0b[:, HALF:S], "s")
-        move(g1[:, HALF:S], pg1b[:, HALF:S], "s")
+        for i in range(2):
+            nodes = slice(i * HALF, (i + 1) * HALF)
+            nc.vector.tensor_copy(xq_w[:, nodes], xw.bitcast(U32).indirect(offs_t[:, 16 * i : 16 * i + 16]))
+            move(g0[:, nodes], product(q10, "b%d" % i, 0, (i,))[:, nodes], "s")
+        q11 = quantize(c11, "g1")
+        for i in range(2):
+            nodes = slice(i * HALF, (i + 1) * HALF)
+            move(g1[:, nodes], product(q11, "b%d" % (2 + i), 0, (i,))[:, nodes], "s")
         c30 = cast(w3_raw[:, :, 0:P], "c30", "v")
         c31 = cast(w3_raw[:, :, P:N], "c31", "v")
         ph0 = whole(quantize(c30, "h0", "h0_codes"), "b4")
@@ -236,4 +237,4 @@ def tile_picked_filmg_silu_p_kernel(
         o1 = new("o1", V)
         for c in range(2):
             nc.vector.tensor_tensor(o1[:, cols[c]], sum1[c], act[c], ADD)
-            nc.sync.dma_start(out[P:N, cols[c]], o1[:, cols[c]])
+        nc.sync.dma_start(out[P:N, :], o1)

@@ -130,14 +130,14 @@ def tile_picked_filmg_silu_p_kernel(
             return t
 
         xs = new("xs", T, U8)
-        offs_t = load_list(offs, "offs_t")
         xs_rows = new("xs_rows", T // 4, I32)
         nc.vector.memset(xs.bitcast(I32), 0)
         for q in range(4):
             live = slice(32 * q, 32 * q + 4)
-            eng = nc.scalar if q % 2 == 0 else nc.sync
+            eng = nc.sync if q % 2 == 0 else nc.scalar
             eng.dma_start(xs_rows[live, :], x_scales[0, 4 * q : 4 * q + 4, :].bitcast(I32))
             nc.vector.tensor_copy(xs.bitcast(I32)[live, :], xs_rows[live, :])
+        offs_t = load_list(offs, "offs_t")
         w1_raw = [load_w(w1[:, 0:P], "w10_raw")]
         xw = new("xw", T, I32)
         nc.sync.dma_start(xw, x_words[0].rearrange("p n t -> p (n t)").bitcast(I32))

@@ -135,8 +135,12 @@ def tile_picked_filmg_silu_p_kernel(
         for q in range(4):
             live = slice(32 * q, 32 * q + 4)
             eng = nc.sync if q % 2 == 0 else nc.scalar
-            eng.dma_start(xs_rows[live, :], x_scales[0, 4 * q : 4 * q + 4, :].bitcast(I32))
-            nc.vector.tensor_copy(xs.bitcast(I32)[live, :], xs_rows[live, :])
+            rows = x_scales[0, 4 * q : 4 * q + 4, :].bitcast(I32)
+            if q < 3:
+                eng.dma_start(xs_rows[live, :], rows)
+                nc.vector.tensor_copy(xs.bitcast(I32)[live, :], xs_rows[live, :])
+            else:
+                eng.dma_start(xs.bitcast(I32)[live, :], rows)
         offs_t = load_list(offs, "offs_t")
         w1_raw = [load_w(w1[:, 0:P], "w10_raw")]
         xw = new("xw", T, I32)
@@ -152,7 +156,8 @@ def tile_picked_filmg_silu_p_kernel(
         nc.scalar.activation(warm[:, 4:5], warm[:, 0:1], SILU)
 
         ident = keep.tile([P, P], F32, name="ident")
-        make_identity(nc, ident[:])
+        nc.vector.memset(ident[:], 0.0)
+        make_identity(nc, ident[:], nomemset=True)
 
         xq_s = new("xq_s", S, U8)
         nc.vector.tensor_copy(xq_s, xs.indirect(offs_t[:]))

@@ -190,9 +190,12 @@ def tile_picked_filmg_silu_p_kernel(
         h1 = empty(ph1, "h1", "v", "c20")
         ps1 = whole(q21, "b5")
         s0 = empty(ps0, "s0", "s")
-        product(q20, "b6", 0, (0,))
+        nc.tensor.matmul_mx(
+            out=bank("b6")[:, 0:P], lhsT=q20[0].bitcast(FP8X4), lhsT_scale=q20[1],
+            rhs=xq_w[:, 0:P].bitcast(FP8X4), rhs_scale=xq_s[:, 0:P], start=True, stop=True,
+        )
         s1 = empty(ps1, "s1", "s")
-        whole(q20, "b5")
+        product(q20, "b5", 0, (0,))
         tt = keep.tile([P, 2 * D, V], F32, name="tt", tag="w2_raw", align_bytes=64)
         t = [[tt[:, m * D + d, :] for d in range(D)] for m in range(2)]
         scaled(h0, gc0, t[0])

@@ -190,12 +190,18 @@ def tile_picked_filmg_silu_p_kernel(
         h1 = empty(ph1, "h1", "v", "c20")
         ps1 = whole(q21, "b5")
         s0 = empty(ps0, "s0", "s")
-        nc.tensor.matmul_mx(
-            out=bank("b6")[:, 0:P], lhsT=q20[0].bitcast(FP8X4), lhsT_scale=q20[1],
-            rhs=xq_w[:, 0:P].bitcast(FP8X4), rhs_scale=xq_s[:, 0:P], start=True, stop=True,
-        )
+
+        def warm_up(dst):
+            nc.tensor.matmul_mx(
+                out=dst, lhsT=q20[0].bitcast(FP8X4), lhsT_scale=q20[1],
+                rhs=q11[0].bitcast(FP8X4), rhs_scale=q11[1], start=True, stop=True,
+            )
+
+        warm_up(bank("b6")[:, 0:P])
         s1 = empty(ps1, "s1", "s")
-        product(q20, "b5", 0, (0,))
+        spare = bank("b5")
+        for c in range(2):
+            warm_up(spare[:, c * P : (c + 1) * P])
         tt = keep.tile([P, 2 * D, V], F32, name="tt", tag="w2_raw", align_bytes=64)
         t = [[tt[:, m * D + d, :] for d in range(D)] for m in range(2)]
         scaled(h0, gc0, t[0])

from contextlib import ExitStack

import concourse.mybir as mybir
from concourse.masks import make_identity

K, T, S, V, N = 512, 1024, 512, 256, 256
P = 128
PACK = 4
D = 3
HALF = S // 2
FLOPS = 3 * 2 * K * N * S

F32 = mybir.dt.float32
BF16 = mybir.dt.bfloat16
I32 = mybir.dt.int32
U32 = mybir.dt.uint32
U16 = mybir.dt.uint16
U8 = mybir.dt.uint8
FP8X4 = mybir.dt.float8_e4m3fn_x4
MULT = mybir.AluOpType.mult
ADD = mybir.AluOpType.add
SILU = mybir.ActivationFunctionType.Silu
COPY = mybir.ActivationFunctionType.Copy


def tile_picked_filmg_silu_p_kernel(
    tc, x_words, x_scales, w1, w2, w3, offs, cen, pos1, pos2, pos3, out
):
    nc = tc.nc
    with ExitStack() as ctx:
        keep = ctx.enter_context(tc.tile_pool(name="keep", bufs=1))
        banks = ctx.enter_context(tc.psum_pool(name="banks", bufs=1))

        def new(name, width, dtype=F32, tag=None):
            return keep.tile([P, width], dtype, name=name, tag=tag or name, align_bytes=64)[:]

        def load_list(src, name):
            t = keep.tile(list(src.shape), U16, name=name)
            nc.sync.dma_start(t[:], src)
            return t

        def load_w(w, name, eng=nc.sync):
            t = keep.tile([P, PACK, w.shape[1]], F32, name=name, tag=name, align_bytes=64)
            eng.dma_start(t[:], w.rearrange("(p j) n -> p j n", j=PACK))
            return t

        def cast(raw, name, eng, tag=None):
            t = keep.tile([P, raw.shape[2], PACK], BF16, name=name, tag=tag or name, align_bytes=64)
            dst = t[:].rearrange("p (c i) j -> p c j i", i=4)
            src = raw.rearrange("p j (c i) -> p c j i", i=4)
            if eng == "v":
                nc.vector.tensor_copy(dst, src)
            elif eng == "s":
                nc.scalar.copy(dst, src)
            else:
                nc.gpsimd.tensor_scalar(dst, src, 1.0, 0.0, MULT, ADD)
            return t

        def quantize(grouped, name, tag=None):
            codes = new(name + "_codes", grouped.shape[1], U32, tag)
            scales = new(name + "_scales", grouped.shape[1], U8)
            nc.vector.quantize_mx(
                out=codes.bitcast(FP8X4), scales=scales, in_=grouped[:].rearrange("p c j -> p (c j)")
            )
            return codes, scales

        def bank(tag):
            return banks.tile([P, S], F32, name=tag, tag=tag)

        def product(q, tag, lo=0, halves=(0, 1)):
            acc = bank(tag)
            for i in halves:
                nc.tensor.matmul_mx(
                    out=acc[:, i * HALF : (i + 1) * HALF],
                    lhsT=q[0][:, lo : lo + P].bitcast(FP8X4), lhsT_scale=q[1][:, lo : lo + P],
                    rhs=xq_w[:, i * HALF : (i + 1) * HALF].bitcast(FP8X4), rhs_scale=xq_s[:, i * HALF : (i + 1) * HALF],
                    start=True, stop=True,
                )
            return acc

        def whole(q, tag, lo=0):
            acc = bank(tag)
            nc.tensor.matmul_mx(
                out=acc[:], lhsT=q[0][:, lo : lo + P].bitcast(FP8X4), lhsT_scale=q[1][:, lo : lo + P],
                rhs=xq_w.bitcast(FP8X4), rhs_scale=xq_s, start=True, stop=True,
            )
            return acc

        def move(dst, src, eng):
            if eng == "v":
                nc.vector.tensor_copy(dst, src)
            else:
                nc.scalar.copy(dst, src)

        def empty(acc, name, eng, tag=None):
            res = new(name, S, F32, tag)
            if eng == "v":
                nc.vector.tensor_copy(res, acc[:])
            else:
                nc.scalar.copy(res, acc[:])
            return res

        def fetch(res, name, eng, tag=None):
            t = new(name, V, F32, tag)
            if eng == "v":
                nc.vector.tensor_copy(t, res.indirect(cen_t[:]))
            else:
                nc.scalar.activation(t, res.indirect(cen_t[:]), COPY)
            return t

        def scaled(h, gc, t):
            for d in range(D):
                nc.vector.tensor_tensor(t[d], h.indirect(pos_t[d][:]), gc, MULT)

        def turn(dst, src, start, stop):
            for c in range(2):
                nc.tensor.matmul(
                    dst[:, c * P : (c + 1) * P], src[:, c * P : (c + 1) * P], ident[:],
                    start=start and c == 0, stop=stop and c == 1, is_transpose=True,
                )

        def silu(src, name, tag=None):
            t = new(name, src.shape[1], F32, tag)
            nc.scalar.activation(t, src, SILU)
            return t

        def add(a, b, name, tag=None):
            t = new(name, a.shape[1], F32, tag)
            nc.vector.tensor_tensor(t, a, b, ADD)
            return t

        xs = new("xs", T, U8)
        xs_rows = new("xs_rows", T // 4, I32)
        nc.vector.memset(xs.bitcast(I32), 0)
        for q in range(4):
            live = slice(32 * q, 32 * q + 4)
            eng = nc.sync if q % 2 == 0 else nc.scalar
            rows = x_scales[0, 4 * q : 4 * q + 4, :].bitcast(I32)
            if q < 3:
                eng.dma_start(xs_rows[live, :], rows)
                nc.vector.tensor_copy(xs.bitcast(I32)[live, :], xs_rows[live, :])
            else:
                eng.dma_start(xs.bitcast(I32)[live, :], rows)
        offs_t = load_list(offs, "offs_t")
        w1_raw = [load_w(w1[:, 0:P], "w10_raw")]
        xw = new("xw", T, I32)
        nc.sync.dma_start(xw, x_words[0].rearrange("p n t -> p (n t)").bitcast(I32))
        w1_raw.append(load_w(w1[:, P:N], "w11_raw"))
        w3_raw = load_w(w3, "w3_raw")
        cen_t = load_list(cen, "cen_t")
        w2_raw = load_w(w2, "w2_raw")
        pos_t = [load_list(pos1, "pos1_t"), load_list(pos2, "pos2_t"), load_list(pos3, "pos3_t")]

        warm = keep.tile([P, 8], F32, name="warm")
        nc.vector.memset(warm[:, 0:1], 0.0)
        nc.scalar.activation(warm[:, 4:5], warm[:, 0:1], SILU)

        ident = keep.tile([P, P], F32, name="ident")
        nc.vector.memset(ident[:], 0.0)
        make_identity(nc, ident[:], nomemset=True)

        xq_s = new("xq_s", S, U8)
        nc.vector.tensor_copy(xq_s, xs.indirect(offs_t[:]))
        c10 = cast(w1_raw[0][:], "c10", "s")
        c11 = cast(w1_raw[1][:], "c11", "s")
        q10 = quantize(c10, "g0")
        xq_w = new("xq_w", S, U32)
        g0 = new("g0", S)
        g1 = new("g1", S)
        for i in range(2):
            nodes = slice(i * HALF, (i + 1) * HALF)
            nc.vector.tensor_copy(xq_w[:, nodes], xw.bitcast(U32).indirect(offs_t[:, 16 * i : 16 * i + 16]))
            move(g0[:, nodes], product(q10, "b%d" % i, 0, (i,))[:, nodes], "s")
        q11 = quantize(c11, "g1")
        for i in range(2):
            nodes = slice(i * HALF, (i + 1) * HALF)
            move(g1[:, nodes], product(q11, "b%d" % (2 + i), 0, (i,))[:, nodes], "s")
        c30 = cast(w3_raw[:, :, 0:P], "c30", "v")
        c31 = cast(w3_raw[:, :, P:N], "c31", "v")
        ph0 = whole(quantize(c30, "h0", "h0_codes"), "b4")
        ph1 = whole(quantize(c31, "h1"), "b5")
        gc0 = fetch(g0, "gc0", "s")
        h0 = empty(ph0, "h0", "s")
        gc1 = fetch(g1, "gc1", "s", "h0_codes")
        c20 = cast(w2_raw[:, :, 0:P], "c20", "v")
        c21 = cast(w2_raw[:, :, P:N], "c21", "v")
        q20 = quantize(c20, "s0")
        q21 = quantize(c21, "s1", "s1_codes")
        ps0 = whole(q20, "b6")
        h1 = empty(ph1, "h1", "v", "c20")
        ps1 = whole(q21, "b5")
        s0 = empty(ps0, "s0", "s")

        def warm_up(dst):
            nc.tensor.matmul_mx(
                out=dst, lhsT=q20[0].bitcast(FP8X4), lhsT_scale=q20[1],
                rhs=q11[0].bitcast(FP8X4), rhs_scale=q11[1], start=True, stop=True,
            )

        warm_up(bank("b6")[:, 0:P])
        s1 = empty(ps1, "s1", "s")
        spare = bank("b5")
        for c in range(2):
            warm_up(spare[:, c * P : (c + 1) * P])
        tt = keep.tile([P, 2 * D, V], F32, name="tt", tag="w2_raw", align_bytes=64)
        t = [[tt[:, m * D + d, :] for d in range(D)] for m in range(2)]
        scaled(h0, gc0, t[0])
        sc = [fetch(s0, "sc0", "s", "s1_codes"), fetch(s1, "sc1", "s")]
        cols = [slice(c * P, (c + 1) * P) for c in range(2)]
        nc.vector.tensor_tensor(t[1][0], h1.indirect(pos_t[0][:]), gc1, MULT)
        for d in range(1, D):
            for c in range(2):
                nc.vector.tensor_tensor(
                    t[1][d][:, cols[c]], h1.indirect(pos_t[d][:, 8 * c : 8 * c + 8]), gc1[:, cols[c]], MULT
                )

        def flip(dst, src, start, stop):
            nc.tensor.matmul(dst, src, ident[:], start=start, stop=stop, is_transpose=True)

        def through(m, d, tag):
            u = bank(tag)
            first, second = (t[m][d], sc[m]) if m == 0 and d < D - 1 else (sc[m], t[m][d])
            turn(u, first, True, False)
            turn(u, second, False, True)
            return silu(u[:, 0:V], "a%d%d" % (m, d))

        a0 = [through(0, d, "b%d" % d) for d in range(D)]
        a10 = through(1, 0, "b3")
        a11 = []
        for c in range(2):
            u = bank("b%d" % (4 + c))[:, 0:P]
            flip(u, sc[1][:, cols[c]], True, False)
            flip(u, t[1][1][:, cols[c]], False, True)
            a11.append(silu(u, "a11%d" % c))
        sum0 = bank("b0")[:, 0:V]
        for d in range(D):
            turn(sum0, a0[d], d == 0, d == D - 1)
        o0 = new("o0", V)
        nc.vector.tensor_copy(o0, sum0)
        nc.sync.dma_start(out[0:P, :], o0)
        pre = new("pre", V)
        act = [t[1][1][:, cols[1]], a10[:, cols[0]]]
        for c in range(2):
            nc.vector.tensor_tensor(pre[:, cols[c]], t[1][D - 1][:, cols[c]], sc[1][:, cols[c]], ADD)
        sum1 = [bank("b%d" % (6 + c))[:, 0:P] for c in range(2)]
        for c in range(2):
            flip(sum1[c], a10[:, cols[c]], True, False)
            flip(sum1[c], a11[c], False, True)
        for c in range(2):
            nc.scalar.activation(act[c], pre[:, cols[c]], SILU)
        o1 = new("o1", V)
        for c in range(2):
            nc.vector.tensor_tensor(o1[:, cols[c]], sum1[c], act[c], ADD)
        nc.sync.dma_start(out[P:N, :], o1)
